import numpy as np, ml_dtypes
CORES = [7,15,23,39,47,63,71,79,87,95,119,127]
N = 12
F = 256
GROUPS = [[0,1,2],[3,4,5],[6,7,8],[9,10,11]]
def setup_inputs(rng):
    return {"x": rng.standard_normal((N, 128, F), dtype=np.float32).astype(ml_dtypes.bfloat16), "w": (rng.standard_normal((N, 128, 128), dtype=np.float32) / 11).astype(ml_dtypes.bfloat16)}
def setup_inputs_big(rng):
    d = setup_inputs(rng)
    for k in ("x", "w"): d[k] = (d[k].astype(np.float32) * 1024.0).astype(d[k].dtype)
    return d
def setup_inputs_small(rng):
    d = setup_inputs(rng)
    for k in ("x", "w"): d[k] = (d[k].astype(np.float32) * (1 / 1024.0)).astype(d[k].dtype)
    return d
def setup_inputs_apart(rng):
    d = setup_inputs(rng)
    f = (10.0 ** rng.permutation(np.linspace(-1.5, 1.5, N))).astype(np.float32).reshape(N, 1, 1)
    for k in ("x", "w"): d[k] = (d[k].astype(np.float32) * f).astype(d[k].dtype)
    return d
def reference(x, w):
    X, W = x.astype(np.float64), w.astype(np.float64)
    s = sum(W[g[0]].T @ np.maximum(sum(X[j] for j in g), 0.0) for g in GROUPS).astype(ml_dtypes.bfloat16)
    return {"y": np.broadcast_to(s, (N,) + s.shape)}

@@ -1,0 +1,176 @@
+from concourse.bass import DstId, RemoteDMATransfer
+from concourse.mybir import AluOpType
+
+F = 256
+M = 128
+
+SCRATCH = {
+    "xs0": ("sbuf", [128, F + M], "bfloat16"),
+    "xs1": ("sbuf", [128, F], "bfloat16"),
+    "xs2": ("sbuf", [128, F], "bfloat16"),
+    "zero": ("sbuf", [128, F], "bfloat16"),
+    "t": ("sbuf", [128, F], "bfloat16"),
+    "p": ("sbuf", [128, F], "bfloat16"),
+    "pin0": ("sbuf", [128, F], "bfloat16"),
+    "pin1": ("sbuf", [128, F], "bfloat16"),
+    "pin2": ("sbuf", [128, F], "bfloat16"),
+    "pin3": ("sbuf", [128, F], "bfloat16"),
+    "ysb": ("sbuf", [128, F], "bfloat16"),
+    "psx0": ("psum", [128, 512], "float32"),
+    "psx1": ("psum", [128, 512], "float32"),
+    "psp": ("psum", [128, 512], "float32"),
+    "psf0": ("psum", [128, 512], "float32"),
+    "psf1": ("psum", [128, 512], "float32"),
+}
+SEMAPHORES = ["ldx", "ldw", "ax0", "ax1", "ax2", "zf", "vx0", "vx1", "vt", "mm", "pc",
+              "ap0", "ap1", "ap2", "ap3", "vf0", "vf1", "vf2", "st", "sent"]
+
+
+def _route(topo, a, b):
+    ca, cb, d = topo.chip(a), topo.chip(b), topo.die(a)
+    if ca == cb:
+        return []
+    if topo.same_plane(ca, cb):
+        return [("out", ca, d), ("in", cb, d)]
+    mate = [k for k in range(topo.CHIPS) if topo.mates(ca, k)][0]
+    way = [("mate", ca, mate, d)]
+    if mate != cb:
+        way += [("out", mate, d), ("in", cb, d)]
+    return way
+
+
+def _perms(items):
+    if len(items) <= 1:
+        return [list(items)]
+    return [[items[i]] + rest for i in range(len(items)) for rest in _perms(items[:i] + items[i + 1:])]
+
+
+def _exchange_sets(groups, cores, topo):
+    best = [None, None]
+
+    def cost(rows):
+        total, load = 0, {}
+        for s in range(len(rows[0])):
+            members = [cores[row[s]] for row in rows]
+            for a in members:
+                for b in members:
+                    if a != b:
+                        for link in _route(topo, a, b):
+                            total += 1
+                            load[link] = load.get(link, 0) + 1
+        return (total, max(load.values()) if load else 0)
+
+    def search(rows):
+        if len(rows) == len(groups):
+            c = cost(rows)
+            if best[0] is None or c < best[0]:
+                best[0], best[1] = c, [list(r) for r in rows]
+            return
+        options = _perms(list(groups[len(rows)])) if rows else [list(groups[0])]
+        for o in options:
+            search(rows + [o])
+
+    search([])
+    rows = best[1]
+    return [[row[s] for row in rows] for s in range(len(rows[0]))]
+
+
+def _send(g, core, T, topo, dst_cores, src, dst, remote_sem):
+    mask = None
+    ids = []
+    for d in dst_cores:
+        assert topo.may_write(core, d)
+        mask = topo.mask(core, d) if mask is None else (mask & topo.mask(core, d))
+        rid, pid, _se = topo.addr(d)
+        ids.append(DstId(rid=rid, pnc=pid))
+    tr = RemoteDMATransfer(dst_ids=ids, dma_engine_mask=mask, remote_sem=remote_sem,
+                           srcs=[src], dsts=[dst for _d in dst_cores], alu_op=0)
+    g.remote_dma_fused([tr], local_sem=T.sem.sent)
+    return bin(mask).count("1")
+
+
+def rank_program(g, core, T, topo):
+    rank = T.rank_of(core)
+    if rank is None:
+        return
+    groups = T.tables["GROUPS"]
+    cores = T.cores
+    gi = [k for k in range(len(groups)) if rank in groups[k]][0]
+    grp = groups[gi]
+    n = len(grp)
+    mi = grp.index(rank)
+    ng = len(groups)
+    xset = [s for s in _exchange_sets(groups, cores, topo) if rank in s][0]
+    add, vmax = AluOpType.add, AluOpType.max
+    V, PE = g.vector, g.tensor
+
+    def engines(src_rank, dst_ranks):
+        m = None
+        for d in dst_ranks:
+            k = topo.mask(cores[src_rank], cores[d])
+            m = k if m is None else (m & k)
+        return bin(m).count("1")
+
+    xs = [T["xs%d" % k] for k in range(n)]
+    own = xs[mi]
+
+    g.sync.dma_start(own[:, 0:F], T.x[:]).then_inc(T.sem.ldx, 16)
+    if mi == 0:
+        g.scalar.dma_start(own[:, F:F + M], T.w[:]).then_inc(T.sem.ldw, 16)
+    V.memset(T.zero[:], 0.0).then_inc(T.sem.zf, 1)
+
+    g.wait_ge(T.sem.ldx, 16)
+    if mi == 0:
+        g.wait_ge(T.sem.ldw, 16)
+    width = F + M if mi == 0 else F
+    others = [grp[(mi + k) % n] for k in range(1, n)]
+    sent = _send(g, core, T, topo, [cores[r] for r in others], own[:, 0:width], own[:, 0:width],
+                 T.sem["ax%d" % mi])
+
+    V.wait_ge(T.sem.ldx, 16)
+    acc = own[:, 0:F]
+    psx = [T.psx0, T.psx1]
+    for k in range(1, n):
+        j = (mi - k) % n
+        peers = [grp[(j + q) % n] for q in range(1, n)]
+        V.wait_ge(T.sem["ax%d" % j], engines(grp[j], peers))
+        if k > 1:
+            V.wait_ge(T.sem["vx%d" % (k - 2)], 1)
+        out = psx[(k - 1) % 2][:, 0:F]
+        V.tensor_tensor(out, acc, xs[j][:, 0:F], add).then_inc(T.sem["vx%d" % (k - 1)], 1)
+        acc = out
+    V.wait_ge(T.sem["vx%d" % (n - 2)], 1)
+    V.wait_ge(T.sem.zf, 1)
+    V.tensor_tensor(T.t[:], acc, T.zero[:], vmax).then_inc(T.sem.vt, 1)
+
+    if mi == 0:
+        PE.wait_ge(T.sem.ldw, 16)
+    else:
+        PE.wait_ge(T.sem.ax0, engines(grp[0], [r for r in grp if r != grp[0]]))
+    PE.wait_ge(T.sem.vt, 1)
+    PE.matmul(T.psp[:, 0:F], xs[0][:, F:F + M], T.t[:], True, True).then_inc(T.sem.mm, 1)
+    V.wait_ge(T.sem.mm, 1)
+    V.tensor_copy(T.p[:], T.psp[:, 0:F]).then_inc(T.sem.pc, 1)
+
+    g.wait_ge(T.sem.pc, 1)
+    partners = [xset[(gi + k) % ng] for k in range(1, ng)]
+    pin_own = T["pin%d" % gi]
+    sent += _send(g, core, T, topo, [cores[r] for r in partners], T.p[:], pin_own[:], T.sem["ap%d" % gi])
+
+    V.wait_ge(T.sem.pc, 1)
+    acc = T.psp[:, 0:F]
+    psf = [T.psf0, T.psf1]
+    for k in range(1, ng):
+        h = (gi - k) % ng
+        peers = [xset[(h + q) % ng] for q in range(1, ng)]
+        V.wait_ge(T.sem["ap%d" % h], engines(xset[h], peers))
+        if k > 1:
+            V.wait_ge(T.sem["vf%d" % (k - 2)], 1)
+        out = T.ysb[:] if k == ng - 1 else psf[(k - 1) % 2][:, 0:F]
+        V.tensor_tensor(out, acc, T["pin%d" % h][:], add).then_inc(T.sem["vf%d" % (k - 1)], 1)
+        acc = out
+
+    g.sync.wait_ge(T.sem["vf%d" % (ng - 2)], 1)
+    g.sync.dma_start(T.y[:], T.ysb[:]).then_inc(T.sem.st, 16)
+    g.sync.wait_ge(T.sem.st, 16)
+    g.wait_ge(T.sem.sent, sent)

@@ -2,6 +2,7 @@ from concourse.bass import DstId, RemoteDMATransfer
 from concourse.mybir import AluOpType
 
 F = 256
+H = F // 2
 M = 128
 
 SCRATCH = {
@@ -9,21 +10,23 @@ SCRATCH = {
     "xs1": ("sbuf", [128, F], "bfloat16"),
     "xs2": ("sbuf", [128, F], "bfloat16"),
     "zero": ("sbuf", [128, F], "bfloat16"),
-    "t": ("sbuf", [128, F], "bfloat16"),
+    "s1": ("sbuf", [128, F], "bfloat16"),
+    "q": ("sbuf", [128, F], "bfloat16"),
     "p": ("sbuf", [128, F], "bfloat16"),
     "pin0": ("sbuf", [128, F], "bfloat16"),
     "pin1": ("sbuf", [128, F], "bfloat16"),
     "pin2": ("sbuf", [128, F], "bfloat16"),
     "pin3": ("sbuf", [128, F], "bfloat16"),
     "ysb": ("sbuf", [128, F], "bfloat16"),
-    "psx0": ("psum", [128, 512], "float32"),
-    "psx1": ("psum", [128, 512], "float32"),
-    "psp": ("psum", [128, 512], "float32"),
+    "psnx": ("psum", [128, 512], "float32"),
+    "psn": ("psum", [128, 512], "float32"),
+    "psp0": ("psum", [128, 512], "float32"),
+    "psp1": ("psum", [128, 512], "float32"),
     "psf0": ("psum", [128, 512], "float32"),
     "psf1": ("psum", [128, 512], "float32"),
 }
-SEMAPHORES = ["ldx", "ldw", "ax0", "ax1", "ax2", "zf", "vx0", "vx1", "vt", "mm", "pc",
-              "ap0", "ap1", "ap2", "ap3", "vf0", "vf1", "vf2", "st", "sent"]
+SEMAPHORES = ["ldx", "ldw", "ax0", "ax1", "ax2", "zf", "vnx", "vn", "vs", "vq0", "vq1", "mm0", "mm1", "pc0", "pc1",
+              "ap0", "ap1", "ap2", "ap3", "vfa", "vfb", "vf1", "vf2", "st", "sent"]
 
 
 def _route(topo, a, b):
@@ -75,18 +78,24 @@ def _exchange_sets(groups, cores, topo):
     return [[row[s] for row in rows] for s in range(len(rows[0]))]
 
 
+def _mask(topo, src, dst_cores):
+    m = None
+    for d in dst_cores:
+        assert topo.may_write(src, d)
+        m = topo.mask(src, d) if m is None else (m & topo.mask(src, d))
+    return m, bin(m).count("1")
+
+
 def _send(g, core, T, topo, dst_cores, src, dst, remote_sem):
-    mask = None
+    mask, count = _mask(topo, core, dst_cores)
     ids = []
     for d in dst_cores:
-        assert topo.may_write(core, d)
-        mask = topo.mask(core, d) if mask is None else (mask & topo.mask(core, d))
         rid, pid, _se = topo.addr(d)
         ids.append(DstId(rid=rid, pnc=pid))
     tr = RemoteDMATransfer(dst_ids=ids, dma_engine_mask=mask, remote_sem=remote_sem,
                            srcs=[src], dsts=[dst for _d in dst_cores], alu_op=0)
     g.remote_dma_fused([tr], local_sem=T.sem.sent)
-    return bin(mask).count("1")
+    return count
 
 
 def rank_program(g, core, T, topo):
@@ -100,77 +109,87 @@ def rank_program(g, core, T, topo):
     n = len(grp)
     mi = grp.index(rank)
     ng = len(groups)
+    assert n == 3 and ng == 4
     xset = [s for s in _exchange_sets(groups, cores, topo) if rank in s][0]
-    add, vmax = AluOpType.add, AluOpType.max
+    add, sub, vmax = AluOpType.add, AluOpType.subtract, AluOpType.max
     V, PE = g.vector, g.tensor
+    sem = T.sem
 
     def engines(src_rank, dst_ranks):
-        m = None
-        for d in dst_ranks:
-            k = topo.mask(cores[src_rank], cores[d])
-            m = k if m is None else (m & k)
-        return bin(m).count("1")
+        return _mask(topo, cores[src_rank], [cores[d] for d in dst_ranks])[1]
+
+    def x_count(j):
+        return engines(grp[j], [grp[(j + k) % n] for k in range(1, n)])
+
+    def p_count(h):
+        return engines(xset[h], [xset[(h + k) % ng] for k in range(1, ng)])
 
     xs = [T["xs%d" % k] for k in range(n)]
     own = xs[mi]
+    W = xs[0][:, F:F + M]
+    halves = [(0, H), (H, F)]
+    psp = [T.psp0, T.psp1]
 
-    g.sync.dma_start(own[:, 0:F], T.x[:]).then_inc(T.sem.ldx, 16)
+    g.sync.dma_start(own[:, 0:F], T.x[:]).then_inc(sem.ldx, 16)
     if mi == 0:
-        g.scalar.dma_start(own[:, F:F + M], T.w[:]).then_inc(T.sem.ldw, 16)
-    V.memset(T.zero[:], 0.0).then_inc(T.sem.zf, 1)
+        g.scalar.dma_start(own[:, F:F + M], T.w[:]).then_inc(sem.ldw, 16)
+    V.memset(T.zero[:], 0.0).then_inc(sem.zf, 1)
 
-    g.wait_ge(T.sem.ldx, 16)
+    g.wait_ge(sem.ldx, 16)
     if mi == 0:
-        g.wait_ge(T.sem.ldw, 16)
+        g.wait_ge(sem.ldw, 16)
     width = F + M if mi == 0 else F
     others = [grp[(mi + k) % n] for k in range(1, n)]
     sent = _send(g, core, T, topo, [cores[r] for r in others], own[:, 0:width], own[:, 0:width],
-                 T.sem["ax%d" % mi])
+                 sem["ax%d" % mi])
 
-    V.wait_ge(T.sem.ldx, 16)
-    acc = own[:, 0:F]
-    psx = [T.psx0, T.psx1]
-    for k in range(1, n):
-        j = (mi - k) % n
-        peers = [grp[(j + q) % n] for q in range(1, n)]
-        V.wait_ge(T.sem["ax%d" % j], engines(grp[j], peers))
-        if k > 1:
-            V.wait_ge(T.sem["vx%d" % (k - 2)], 1)
-        out = psx[(k - 1) % 2][:, 0:F]
-        V.tensor_tensor(out, acc, xs[j][:, 0:F], add).then_inc(T.sem["vx%d" % (k - 1)], 1)
-        acc = out
-    V.wait_ge(T.sem["vx%d" % (n - 2)], 1)
-    V.wait_ge(T.sem.zf, 1)
-    V.tensor_tensor(T.t[:], acc, T.zero[:], vmax).then_inc(T.sem.vt, 1)
+    first, last = (mi - 1) % n, (mi - 2) % n
+    V.wait_ge(sem.ldx, 16)
+    V.wait_ge(sem.zf, 1)
+    V.tensor_tensor(T.psnx[:, 0:F], T.zero[:], own[:, 0:F], sub).then_inc(sem.vnx, 1)
+    V.wait_ge(sem["ax%d" % first], x_count(first))
+    V.wait_ge(sem.vnx, 1)
+    V.tensor_tensor(T.psn[:, 0:F], T.psnx[:, 0:F], xs[first][:, 0:F], sub).then_inc(sem.vn, 1)
+    V.wait_ge(sem.vn, 1)
+    V.tensor_tensor(T.s1[:], T.zero[:], T.psn[:, 0:F], sub).then_inc(sem.vs, 1)
+    V.wait_ge(sem["ax%d" % last], x_count(last))
+    for k, (a, b) in enumerate(halves):
+        V.tensor_tensor(T.q[:, a:b], xs[last][:, a:b], T.psn[:, a:b], vmax).then_inc(sem["vq%d" % k], 1)
 
     if mi == 0:
-        PE.wait_ge(T.sem.ldw, 16)
+        PE.wait_ge(sem.ldw, 16)
     else:
-        PE.wait_ge(T.sem.ax0, engines(grp[0], [r for r in grp if r != grp[0]]))
-    PE.wait_ge(T.sem.vt, 1)
-    PE.matmul(T.psp[:, 0:F], xs[0][:, F:F + M], T.t[:], True, True).then_inc(T.sem.mm, 1)
-    V.wait_ge(T.sem.mm, 1)
-    V.tensor_copy(T.p[:], T.psp[:, 0:F]).then_inc(T.sem.pc, 1)
+        PE.wait_ge(sem.ax0, x_count(0))
+    PE.wait_ge(sem.vs, 1)
+    for k, (a, b) in enumerate(halves):
+        PE.matmul(psp[k][:, 0:H], W, T.s1[:, a:b], True, False)
+    for k, (a, b) in enumerate(halves):
+        PE.wait_ge(sem["vq%d" % k], 1)
+        PE.matmul(psp[k][:, 0:H], W, T.q[:, a:b], False, True).then_inc(sem["mm%d" % k], 1)
 
-    g.wait_ge(T.sem.pc, 1)
+    for k, (a, b) in enumerate(halves):
+        V.wait_ge(sem["mm%d" % k], 1)
+        V.tensor_copy(T.p[:, a:b], psp[k][:, 0:H]).then_inc(sem["pc%d" % k], 1)
+
+    g.wait_ge(sem.pc0, 1)
+    g.wait_ge(sem.pc1, 1)
     partners = [xset[(gi + k) % ng] for k in range(1, ng)]
-    pin_own = T["pin%d" % gi]
-    sent += _send(g, core, T, topo, [cores[r] for r in partners], T.p[:], pin_own[:], T.sem["ap%d" % gi])
+    sent += _send(g, core, T, topo, [cores[r] for r in partners], T.p[:], T["pin%d" % gi][:], sem["ap%d" % gi])
 
-    V.wait_ge(T.sem.pc, 1)
-    acc = T.psp[:, 0:F]
-    psf = [T.psf0, T.psf1]
-    for k in range(1, ng):
-        h = (gi - k) % ng
-        peers = [xset[(h + q) % ng] for q in range(1, ng)]
-        V.wait_ge(T.sem["ap%d" % h], engines(xset[h], peers))
-        if k > 1:
-            V.wait_ge(T.sem["vf%d" % (k - 2)], 1)
-        out = T.ysb[:] if k == ng - 1 else psf[(k - 1) % 2][:, 0:F]
-        V.tensor_tensor(out, acc, T["pin%d" % h][:], add).then_inc(T.sem["vf%d" % (k - 1)], 1)
-        acc = out
+    h1, h2, h3 = (gi - 1) % ng, (gi - 2) % ng, (gi - 3) % ng
+    V.wait_ge(sem["ap%d" % h1], p_count(h1))
+    pin = T["pin%d" % h1]
+    V.tensor_tensor(T.psf0[:, 0:H], psp[0][:, 0:H], pin[:, 0:H], add).then_inc(sem.vfa, 1)
+    V.tensor_tensor(T.psf0[:, H:F], psp[1][:, 0:H], pin[:, H:F], add).then_inc(sem.vfb, 1)
+    V.wait_ge(sem["ap%d" % h2], p_count(h2))
+    V.wait_ge(sem.vfa, 1)
+    V.wait_ge(sem.vfb, 1)
+    V.tensor_tensor(T.psf1[:, 0:F], T.psf0[:, 0:F], T["pin%d" % h2][:], add).then_inc(sem.vf1, 1)
+    V.wait_ge(sem["ap%d" % h3], p_count(h3))
+    V.wait_ge(sem.vf1, 1)
+    V.tensor_tensor(T.ysb[:], T.psf1[:, 0:F], T["pin%d" % h3][:], add).then_inc(sem.vf2, 1)
 
-    g.sync.wait_ge(T.sem["vf%d" % (ng - 2)], 1)
-    g.sync.dma_start(T.y[:], T.ysb[:]).then_inc(T.sem.st, 16)
-    g.sync.wait_ge(T.sem.st, 16)
-    g.wait_ge(T.sem.sent, sent)
+    g.sync.wait_ge(sem.vf2, 1)
+    g.sync.dma_start(T.y[:], T.ysb[:]).then_inc(sem.st, 16)
+    g.sync.wait_ge(sem.st, 16)
+    g.wait_ge(sem.sent, sent)

from concourse.bass import DstId, RemoteDMATransfer
from concourse.mybir import AluOpType

F = 256
H = F // 2
M = 128

SCRATCH = {
    "xs0": ("sbuf", [128, F + M], "bfloat16"),
    "xs1": ("sbuf", [128, F], "bfloat16"),
    "xs2": ("sbuf", [128, F], "bfloat16"),
    "zero": ("sbuf", [128, F], "bfloat16"),
    "s1": ("sbuf", [128, F], "bfloat16"),
    "q": ("sbuf", [128, F], "bfloat16"),
    "p": ("sbuf", [128, F], "bfloat16"),
    "pin0": ("sbuf", [128, F], "bfloat16"),
    "pin1": ("sbuf", [128, F], "bfloat16"),
    "pin2": ("sbuf", [128, F], "bfloat16"),
    "pin3": ("sbuf", [128, F], "bfloat16"),
    "ysb": ("sbuf", [128, F], "bfloat16"),
    "psnx": ("psum", [128, 512], "float32"),
    "psn": ("psum", [128, 512], "float32"),
    "psp0": ("psum", [128, 512], "float32"),
    "psp1": ("psum", [128, 512], "float32"),
    "psf0": ("psum", [128, 512], "float32"),
    "psf1": ("psum", [128, 512], "float32"),
}
SEMAPHORES = ["ldx", "ldw", "ax0", "ax1", "ax2", "zf", "vnx", "vn", "vs", "vq0", "vq1", "mm0", "mm1", "pc0", "pc1",
              "ap0", "ap1", "ap2", "ap3", "vfa", "vfb", "vf1", "vf2", "st", "sent"]


def _route(topo, a, b):
    ca, cb, d = topo.chip(a), topo.chip(b), topo.die(a)
    if ca == cb:
        return []
    if topo.same_plane(ca, cb):
        return [("out", ca, d), ("in", cb, d)]
    mate = [k for k in range(topo.CHIPS) if topo.mates(ca, k)][0]
    way = [("mate", ca, mate, d)]
    if mate != cb:
        way += [("out", mate, d), ("in", cb, d)]
    return way


def _perms(items):
    if len(items) <= 1:
        return [list(items)]
    return [[items[i]] + rest for i in range(len(items)) for rest in _perms(items[:i] + items[i + 1:])]


def _exchange_sets(groups, cores, topo):
    best = [None, None]

    def cost(rows):
        total, load = 0, {}
        for s in range(len(rows[0])):
            members = [cores[row[s]] for row in rows]
            for a in members:
                for b in members:
                    if a != b:
                        for link in _route(topo, a, b):
                            total += 1
                            load[link] = load.get(link, 0) + 1
        return (total, max(load.values()) if load else 0)

    def search(rows):
        if len(rows) == len(groups):
            c = cost(rows)
            if best[0] is None or c < best[0]:
                best[0], best[1] = c, [list(r) for r in rows]
            return
        options = _perms(list(groups[len(rows)])) if rows else [list(groups[0])]
        for o in options:
            search(rows + [o])

    search([])
    rows = best[1]
    return [[row[s] for row in rows] for s in range(len(rows[0]))]


def _mask(topo, src, dst_cores):
    m = None
    for d in dst_cores:
        assert topo.may_write(src, d)
        m = topo.mask(src, d) if m is None else (m & topo.mask(src, d))
    return m, bin(m).count("1")


def _send(g, core, T, topo, dst_cores, src, dst, remote_sem):
    mask, count = _mask(topo, core, dst_cores)
    ids = []
    for d in dst_cores:
        rid, pid, _se = topo.addr(d)
        ids.append(DstId(rid=rid, pnc=pid))
    tr = RemoteDMATransfer(dst_ids=ids, dma_engine_mask=mask, remote_sem=remote_sem,
                           srcs=[src], dsts=[dst for _d in dst_cores], alu_op=0)
    g.remote_dma_fused([tr], local_sem=T.sem.sent)
    return count


def rank_program(g, core, T, topo):
    rank = T.rank_of(core)
    if rank is None:
        return
    groups = T.tables["GROUPS"]
    cores = T.cores
    gi = [k for k in range(len(groups)) if rank in groups[k]][0]
    grp = groups[gi]
    n = len(grp)
    mi = grp.index(rank)
    ng = len(groups)
    assert n == 3 and ng == 4
    xset = [s for s in _exchange_sets(groups, cores, topo) if rank in s][0]
    add, sub, vmax = AluOpType.add, AluOpType.subtract, AluOpType.max
    V, PE = g.vector, g.tensor
    sem = T.sem

    def engines(src_rank, dst_ranks):
        return _mask(topo, cores[src_rank], [cores[d] for d in dst_ranks])[1]

    def x_count(j):
        return engines(grp[j], [grp[(j + k) % n] for k in range(1, n)])

    def p_count(h):
        return engines(xset[h], [xset[(h + k) % ng] for k in range(1, ng)])

    xs = [T["xs%d" % k] for k in range(n)]
    own = xs[mi]
    W = xs[0][:, F:F + M]
    halves = [(0, H), (H, F)]
    psp = [T.psp0, T.psp1]

    g.sync.dma_start(own[:, 0:F], T.x[:]).then_inc(sem.ldx, 16)
    if mi == 0:
        g.scalar.dma_start(own[:, F:F + M], T.w[:]).then_inc(sem.ldw, 16)
    V.memset(T.zero[:], 0.0).then_inc(sem.zf, 1)

    g.wait_ge(sem.ldx, 16)
    if mi == 0:
        g.wait_ge(sem.ldw, 16)
    width = F + M if mi == 0 else F
    others = [grp[(mi + k) % n] for k in range(1, n)]
    sent = _send(g, core, T, topo, [cores[r] for r in others], own[:, 0:width], own[:, 0:width],
                 sem["ax%d" % mi])

    first, last = (mi - 1) % n, (mi - 2) % n
    V.wait_ge(sem.ldx, 16)
    V.wait_ge(sem.zf, 1)
    V.tensor_tensor(T.psnx[:, 0:F], T.zero[:], own[:, 0:F], sub).then_inc(sem.vnx, 1)
    V.wait_ge(sem["ax%d" % first], x_count(first))
    V.wait_ge(sem.vnx, 1)
    V.tensor_tensor(T.psn[:, 0:F], T.psnx[:, 0:F], xs[first][:, 0:F], sub).then_inc(sem.vn, 1)
    V.wait_ge(sem.vn, 1)
    V.tensor_tensor(T.s1[:], T.zero[:], T.psn[:, 0:F], sub).then_inc(sem.vs, 1)
    V.wait_ge(sem["ax%d" % last], x_count(last))
    for k, (a, b) in enumerate(halves):
        V.tensor_tensor(T.q[:, a:b], xs[last][:, a:b], T.psn[:, a:b], vmax).then_inc(sem["vq%d" % k], 1)

    if mi == 0:
        PE.wait_ge(sem.ldw, 16)
    else:
        PE.wait_ge(sem.ax0, x_count(0))
    PE.wait_ge(sem.vs, 1)
    for k, (a, b) in enumerate(halves):
        PE.matmul(psp[k][:, 0:H], W, T.s1[:, a:b], True, False)
    for k, (a, b) in enumerate(halves):
        PE.wait_ge(sem["vq%d" % k], 1)
        PE.matmul(psp[k][:, 0:H], W, T.q[:, a:b], False, True).then_inc(sem["mm%d" % k], 1)

    for k, (a, b) in enumerate(halves):
        V.wait_ge(sem["mm%d" % k], 1)
        V.tensor_copy(T.p[:, a:b], psp[k][:, 0:H]).then_inc(sem["pc%d" % k], 1)

    g.wait_ge(sem.pc0, 1)
    g.wait_ge(sem.pc1, 1)
    partners = [xset[(gi + k) % ng] for k in range(1, ng)]
    sent += _send(g, core, T, topo, [cores[r] for r in partners], T.p[:], T["pin%d" % gi][:], sem["ap%d" % gi])

    h1, h2, h3 = (gi - 1) % ng, (gi - 2) % ng, (gi - 3) % ng
    V.wait_ge(sem["ap%d" % h1], p_count(h1))
    pin = T["pin%d" % h1]
    V.tensor_tensor(T.psf0[:, 0:H], psp[0][:, 0:H], pin[:, 0:H], add).then_inc(sem.vfa, 1)
    V.tensor_tensor(T.psf0[:, H:F], psp[1][:, 0:H], pin[:, H:F], add).then_inc(sem.vfb, 1)
    V.wait_ge(sem["ap%d" % h2], p_count(h2))
    V.wait_ge(sem.vfa, 1)
    V.wait_ge(sem.vfb, 1)
    V.tensor_tensor(T.psf1[:, 0:F], T.psf0[:, 0:F], T["pin%d" % h2][:], add).then_inc(sem.vf1, 1)
    V.wait_ge(sem["ap%d" % h3], p_count(h3))
    V.wait_ge(sem.vf1, 1)
    V.tensor_tensor(T.ysb[:], T.psf1[:, 0:F], T["pin%d" % h3][:], add).then_inc(sem.vf2, 1)

    g.sync.wait_ge(sem.vf2, 1)
    g.sync.dma_start(T.y[:], T.ysb[:]).then_inc(sem.st, 16)
    g.sync.wait_ge(sem.st, 16)
    g.wait_ge(sem.sent, sent)
